import numpy as np
CORES = [4,12,20,28,44,60,76,84,92,108,116,124]
N = 12
TK = 512
D = 128 * N
EPS = 0.01
def setup_inputs(rng):
    return {"x": (rng.standard_normal((N, 128, TK), dtype=np.float32) * (0.5 + np.abs(rng.standard_normal((1, 1, TK), dtype=np.float32))) + rng.standard_normal((1, 1, TK), dtype=np.float32)), "w": (rng.standard_normal((N, 128, 128), dtype=np.float32) / 11)}
def setup_inputs_big(rng):
    d = setup_inputs(rng)
    for k in ("x", "w"): d[k] = (d[k].astype(np.float32) * 1048576.0).astype(d[k].dtype)
    return d
def setup_inputs_small(rng):
    d = setup_inputs(rng)
    for k in ("x", "w"): d[k] = (d[k].astype(np.float32) * (1 / 1048576.0)).astype(d[k].dtype)
    return d
def setup_inputs_apart(rng):
    d = setup_inputs(rng)
    f = (10.0 ** rng.permutation(np.linspace(-1.5, 1.5, N))).astype(np.float32).reshape(N, 1, 1)
    for k in ("x", "w"): d[k] = (d[k].astype(np.float32) * f).astype(d[k].dtype)
    return d
def setup_inputs_mixed(rng):
    d = setup_inputs(rng)
    f = (10.0 ** rng.uniform(-3, 3, (1, 1, TK))).astype(np.float32); shape = rng.integers(3, size=(1, 1, TK))
    for k in ("x",):
        x = d[k].astype(np.float32)
        m = x.mean(axis=(0, 1), keepdims=True); level = m + np.sign(x - m) * np.abs(x - m).mean(axis=(0, 1), keepdims=True) * rng.uniform(0.9, 1.1, x.shape).astype(np.float32)
        other = x * np.where(rng.random(x.shape) < 0.5, 0.1, 1.0).astype(np.float32)
        d[k] = (np.where(shape == 1, level, np.where(shape == 2, other, x)) * f).astype(d[k].dtype)
    return d
def reference(x, w):
    X = x.astype(np.float64)
    Z = X
    Z = Z / np.sqrt((Z ** 2).sum(axis=(0, 1)) / D + EPS)
    s = sum(w[r].astype(np.float64).T @ Z[r] for r in range(N)).astype(np.float32)
    return {"y": np.broadcast_to(s, (N,) + s.shape)}

@@ -1,0 +1,197 @@
+from concourse.bass import DstId, RemoteDMATransfer
+from concourse.mybir import AluOpType, ActivationFunctionType
+
+NR = 12
+TK = 512
+DFEAT = 128 * NR
+EPS = 0.01
+NCH = 8
+CW = TK // NCH
+
+SCRATCH = {
+    "xs": ("sbuf", [128, TK], "float32"),
+    "ws": ("sbuf", [128, 128], "float32"),
+    "x2": ("sbuf", [128, TK], "float32"),
+    "ones": ("sbuf", [128, 128], "float32"),
+    "ident": ("sbuf", [128, 128], "float32"),
+    "ps": ("sbuf", [128, TK], "float32"),
+    "qcol": ("sbuf", [128, 4], "float32"),
+    "qland": ("sbuf", [128, 4 * NCH], "float32"),
+    "qeo": ("sbuf", [128, 8], "float32"),
+    "qs": ("sbuf", [128, 4], "float32"),
+    "sq": ("sbuf", [128, 4], "float32"),
+    "sc": ("sbuf", [128, 4], "float32"),
+    "diag": ("sbuf", [128, TK], "float32"),
+    "eo": ("sbuf", [128, 2 * TK], "float32"),
+    "rr": ("sbuf", [128, TK], "float32"),
+    "yo": ("sbuf", [128, TK], "float32"),
+    "pp0": ("psum", [128, 512], "float32"),
+    "pp1": ("psum", [128, 512], "float32"),
+    "pq": ("psum", [128, 512], "float32"),
+    "pS0": ("psum", [128, 512], "float32"),
+    "pS1": ("psum", [128, 512], "float32"),
+    "d1": ("dram", [NCH, 128, CW], "float32"),
+    "lb": ("dram", [NCH, 128, CW], "float32"),
+    "gg": ("dram", [2 * NCH, 128, CW], "float32"),
+}
+SEMAPHORES = ["x0", "x1", "w", "ones", "id", "sq0", "sq1", "pq", "pp0", "pp1", "qc", "ps", "l1", "lsend",
+              "qarrR", "barr", "qarr", "garr0", "garr1", "c1", "c2", "c3", "dg0", "dg1", "dg2", "dg3",
+              "S0", "S1", "l2a", "l2b", "a0", "a1", "m0", "m1", "y0", "y1"]
+
+
+def _layout(T, topo):
+    ranks = list(T.cores)
+    cores = list(range(topo.CHIPS * topo.CORES_PER_CHIP))
+    chips = sorted(set(topo.chip(c) for c in cores))
+    c0 = topo.chip(ranks[0])
+    first = [ch for ch in chips if ch == c0 or topo.same_plane(ch, c0)]
+    planes = [first, [ch for ch in chips if ch not in first]]
+    pranks = [[r for r in ranks if topo.chip(r) in pl] for pl in planes]
+    reducers = []
+    for pi, pl in enumerate(planes):
+        row = []
+        for k, ch in enumerate(pl):
+            cands = [c for c in cores if topo.chip(c) == ch and c not in ranks
+                     and all(topo.may_write(c, r) for r in ranks)]
+            dies = sorted(set(topo.die(c) for c in cands))
+            want = dies[(k + pi) % len(dies)]
+            row.append([c for c in cands if topo.die(c) == want][0])
+        reducers.append(row)
+    return ranks, planes, pranks, reducers
+
+
+def _did(topo, c):
+    rid, pid, _se = topo.addr(c)
+    return DstId(rid=rid, pnc=pid)
+
+
+def _common_mask(topo, src, dsts):
+    m = topo.mask(src, dsts[0])
+    for d in dsts[1:]:
+        m &= topo.mask(src, d)
+    return m
+
+
+def _bits(m):
+    return [1 << b for b in range(16) if (m >> b) & 1]
+
+
+def _reducer(g, core, T, topo, ranks, nsrc, pi, k):
+    S = T.sem
+    qd = [ranks[i] for i in range(k, len(ranks), NCH)]
+    g.wait_ge(S.qarrR, nsrc)
+    g.remote_dma_fused([RemoteDMATransfer(
+        dst_ids=[_did(topo, d) for d in qd], dma_engine_mask=_common_mask(topo, core, ranks), remote_sem=S.qarr,
+        srcs=[T.qland[:, 4 * i:4 * i + 4] for i in range(nsrc)],
+        dsts=[T.qeo[:, 4 * pi:4 * pi + 4] for _ in qd], alu_op=1)], local_sem=S.lsend)
+    order = [ranks[(k + i) % len(ranks)] for i in range(len(ranks))]
+    g.wait_ge(S.barr, nsrc)
+    g.remote_dma_fused([RemoteDMATransfer(
+        dst_ids=[_did(topo, d) for d in order], dma_engine_mask=_common_mask(topo, core, ranks),
+        remote_sem=(S.garr0 if pi == 0 else S.garr1),
+        srcs=[T.lb[i] for i in range(nsrc)],
+        dsts=[T.gg[NCH * pi + k] for _ in order], alu_op=1)], local_sem=S.lsend)
+    g.wait_ge(S.lsend, 2 * len(_bits(_common_mask(topo, core, ranks))))
+
+
+def rank_program(g, core, T, topo):
+    ranks, planes, pranks, reducers = _layout(T, topo)
+    for pi in range(2):
+        if core in reducers[pi]:
+            _reducer(g, core, T, topo, ranks, len(pranks[pi]), pi, reducers[pi].index(core))
+            return
+    if T.rank_of(core) is None:
+        return
+    S = T.sem
+    pi = 0 if core in pranks[0] else 1
+    me = pranks[pi].index(core)
+    red = reducers[pi]
+    eng = _bits(_common_mask(topo, core, red))
+    H = TK // 2
+    mult, add = AluOpType.mult, AluOpType.add
+
+    g.scalar.dma_start(T.xs[:, 0:H], T.x[:, 0:H]).then_inc(S.x0, 16)
+    g.sync.dma_start(T.xs[:, H:TK], T.x[:, H:TK]).then_inc(S.x1, 16)
+    g.scalar.dma_start(T.ws[:, :], T.w[:, :]).then_inc(S.w, 16)
+
+    g.vector.memset(T.ones[:, :], 1.0).then_inc(S.ones, 1)
+    g.wait_ge(S.ones, 1)
+    g.affine_select(T.ident[:, :], T.ones[:, :], [[-1, 128]], AluOpType.is_equal, 0.0, 0, 1).then_inc(S.id, 1)
+
+    g.scalar.wait_ge(S.x0, 16)
+    g.scalar.activation(T.x2[:, 0:H], T.xs[:, 0:H], ActivationFunctionType.Square).then_inc(S.sq0, 1)
+    g.scalar.wait_ge(S.x1, 16)
+    g.scalar.activation(T.x2[:, H:TK], T.xs[:, H:TK], ActivationFunctionType.Square).then_inc(S.sq1, 1)
+
+    g.tensor.wait_ge(S.ones, 1)
+    for j in range(4):
+        if j == 0:
+            g.tensor.wait_ge(S.sq0, 1)
+        if j == 2:
+            g.tensor.wait_ge(S.sq1, 1)
+        g.tensor.matmul(T.pq[:, j:j + 1], T.x2[:, 128 * j:128 * j + 128], T.ones[:, 0:1], True, True).then_inc(S.pq, 1)
+    g.tensor.wait_ge(S.w, 16)
+    g.tensor.wait_ge(S.x0, 16)
+    g.tensor.matmul(T.pp0[:, 0:H], T.ws[:, :], T.xs[:, 0:H], True, True).then_inc(S.pp0, 1)
+    g.tensor.wait_ge(S.x1, 16)
+    g.tensor.matmul(T.pp1[:, 0:H], T.ws[:, :], T.xs[:, H:TK], True, True).then_inc(S.pp1, 1)
+
+    g.vector.wait_ge(S.pq, 4)
+    g.vector.tensor_copy(T.qcol[:, :], T.pq[:, 0:4]).then_inc(S.qc, 1)
+    g.vector.wait_ge(S.pp0, 1)
+    g.vector.tensor_copy(T.ps[:, 0:H], T.pp0[:, 0:H]).then_inc(S.ps, 1)
+    g.vector.wait_ge(S.pp1, 1)
+    g.vector.tensor_copy(T.ps[:, H:TK], T.pp1[:, 0:H]).then_inc(S.ps, 1)
+
+    g.wait_ge(S.qc, 1)
+    g.remote_dma_fused([RemoteDMATransfer(
+        dst_ids=[_did(topo, red[k])], dma_engine_mask=eng[k], remote_sem=S.qarrR,
+        src=T.qcol[:, :], dst=T.qland[:, 4 * me:4 * me + 4]) for k in range(NCH)], local_sem=S.lsend)
+
+    g.sync.wait_ge(S.ps, 2)
+    g.sync.dma_start(T.d1[:, :, :], T.ps[:, :]).then_inc(S.l1, 16)
+    g.wait_ge(S.l1, 16)
+    g.remote_dma_fused([RemoteDMATransfer(
+        dst_ids=[_did(topo, red[k])], dma_engine_mask=eng[k], remote_sem=S.barr,
+        src=T.d1[k], dst=T.lb[me]) for k in range(NCH)], local_sem=S.lsend)
+
+    nq = 2 * len(_bits(_common_mask(topo, reducers[0][0], ranks)))
+    g.vector.wait_ge(S.qarr, nq)
+    g.vector.tensor_tensor(T.qs[:, :], T.qeo[:, 0:4], T.qeo[:, 4:8], add).then_inc(S.c1, 1)
+    g.scalar.wait_ge(S.c1, 1)
+    g.scalar.activation(T.sq[:, :], T.qs[:, :], ActivationFunctionType.Sqrt, bias=EPS, scale=1.0 / DFEAT).then_inc(S.c2, 1)
+    g.vector.wait_ge(S.c2, 1)
+    g.vector.reciprocal(T.sc[:, :], T.sq[:, :]).then_inc(S.c3, 1)
+    g.vector.wait_ge(S.c3, 1)
+    g.vector.wait_ge(S.id, 1)
+    for j in range(4):
+        g.vector.tensor_scalar(T.diag[:, 128 * j:128 * j + 128], T.ident[:, :], T.sc[:, j:j + 1], None,
+                               mult).then_inc(S["dg%d" % j], 1)
+    for j in range(4):
+        g.tensor.wait_ge(S["dg%d" % j], 1)
+        pS = T.pS0 if j < 2 else T.pS1
+        g.tensor.matmul(pS[:, 128 * (j % 2):128 * (j % 2) + 128], T.ones[:, :], T.diag[:, 128 * j:128 * j + 128],
+                        True, True).then_inc(S.S0 if j < 2 else S.S1, 1)
+
+    ng = NCH * len(_bits(_common_mask(topo, reducers[0][0], ranks)))
+    g.sync.wait_ge(S.garr0, ng)
+    g.sync.dma_start(T.eo[:, 0:TK], T.gg[0:NCH]).then_inc(S.l2a, 16)
+    g.scalar.wait_ge(S.garr1, ng)
+    g.scalar.dma_start(T.eo[:, TK:2 * TK], T.gg[NCH:2 * NCH]).then_inc(S.l2b, 16)
+
+    g.vector.wait_ge(S.l2a, 16)
+    g.vector.wait_ge(S.l2b, 16)
+    for h in range(2):
+        lo, hi = h * H, h * H + H
+        g.vector.tensor_tensor(T.rr[:, lo:hi], T.eo[:, lo:hi], T.eo[:, TK + lo:TK + hi], add).then_inc(S["a%d" % h], 1)
+        g.vector.wait_ge(S["a%d" % h], 1)
+        g.vector.wait_ge(S["S%d" % h], 2)
+        g.vector.tensor_tensor(T.yo[:, lo:hi], T.rr[:, lo:hi], (T.pS0 if h == 0 else T.pS1)[:, 0:H],
+                               mult).then_inc(S["m%d" % h], 1)
+    g.sync.wait_ge(S.m0, 1)
+    g.sync.dma_start(T.y[:, 0:H], T.yo[:, 0:H]).then_inc(S.y0, 16)
+    g.scalar.wait_ge(S.m1, 1)
+    g.scalar.dma_start(T.y[:, H:TK], T.yo[:, H:TK]).then_inc(S.y1, 16)
+    g.sync.wait_ge(S.y0, 16)
+    g.scalar.wait_ge(S.y1, 16)
+    g.wait_ge(S.lsend, 2 * NCH)

@@ -3,10 +3,11 @@ from concourse.mybir import AluOpType, ActivationFunctionType
 
 NR = 12
 TK = 512
+H = TK // 2
 DFEAT = 128 * NR
 EPS = 0.01
 NCH = 8
-CW = TK // NCH
+CW = H // NCH
 
 SCRATCH = {
     "xs": ("sbuf", [128, TK], "float32"),
@@ -16,7 +17,6 @@ SCRATCH = {
     "ident": ("sbuf", [128, 128], "float32"),
     "ps": ("sbuf", [128, TK], "float32"),
     "qcol": ("sbuf", [128, 4], "float32"),
-    "qland": ("sbuf", [128, 4 * NCH], "float32"),
     "qeo": ("sbuf", [128, 8], "float32"),
     "qs": ("sbuf", [128, 4], "float32"),
     "sq": ("sbuf", [128, 4], "float32"),
@@ -30,13 +30,16 @@ SCRATCH = {
     "pq": ("psum", [128, 512], "float32"),
     "pS0": ("psum", [128, 512], "float32"),
     "pS1": ("psum", [128, 512], "float32"),
-    "d1": ("dram", [NCH, 128, CW], "float32"),
+    "qd": ("dram", [128, 4], "float32"),
+    "qlb": ("dram", [NCH, 128, 4], "float32"),
+    "qg": ("dram", [2, 128, 4], "float32"),
+    "d1": ("dram", [2 * NCH, 128, CW], "float32"),
     "lb": ("dram", [NCH, 128, CW], "float32"),
-    "gg": ("dram", [2 * NCH, 128, CW], "float32"),
+    "gg": ("dram", [4 * NCH, 128, CW], "float32"),
 }
-SEMAPHORES = ["x0", "x1", "w", "ones", "id", "sq0", "sq1", "pq", "pp0", "pp1", "qc", "ps", "l1", "lsend",
-              "qarrR", "barr", "qarr", "garr0", "garr1", "c1", "c2", "c3", "dg0", "dg1", "dg2", "dg3",
-              "S0", "S1", "l2a", "l2b", "a0", "a1", "m0", "m1", "y0", "y1"]
+SEMAPHORES = ["x0", "x1", "w", "ones", "id", "sq0", "sq1", "pq", "pp0", "pp1", "qc", "lq1", "lq2", "ps0", "ps1",
+              "l10", "l11", "lsend", "qarrR", "barr", "qarr", "g00", "g01", "g10", "g11", "c1", "c2", "c3",
+              "dg0", "dg1", "dg2", "dg3", "S0", "S1", "l20", "l21", "a0", "a1", "m0", "m1", "y0", "y1"]
 
 
 def _layout(T, topo):
@@ -49,14 +52,15 @@ def _layout(T, topo):
     pranks = [[r for r in ranks if topo.chip(r) in pl] for pl in planes]
     reducers = []
     for pi, pl in enumerate(planes):
-        row = []
+        halves = [[], []]
         for k, ch in enumerate(pl):
             cands = [c for c in cores if topo.chip(c) == ch and c not in ranks
                      and all(topo.may_write(c, r) for r in ranks)]
             dies = sorted(set(topo.die(c) for c in cands))
-            want = dies[(k + pi) % len(dies)]
-            row.append([c for c in cands if topo.die(c) == want][0])
-        reducers.append(row)
+            for h in range(2):
+                want = dies[(k + pi + h) % len(dies)]
+                halves[h].append([c for c in cands if topo.die(c) == want][0])
+        reducers.append(halves)
     return ranks, planes, pranks, reducers
 
 
@@ -76,38 +80,49 @@ def _bits(m):
     return [1 << b for b in range(16) if (m >> b) & 1]
 
 
-def _reducer(g, core, T, topo, ranks, nsrc, pi, k):
+def _qserver(h, k):
+    i = (1 - h) * NCH + k
+    return i if i < NR else None
+
+
+def _reducer(g, core, T, topo, ranks, psrc, pi, h, k):
     S = T.sem
-    qd = [ranks[i] for i in range(k, len(ranks), NCH)]
-    g.wait_ge(S.qarrR, nsrc)
-    g.remote_dma_fused([RemoteDMATransfer(
-        dst_ids=[_did(topo, d) for d in qd], dma_engine_mask=_common_mask(topo, core, ranks), remote_sem=S.qarr,
-        srcs=[T.qland[:, 4 * i:4 * i + 4] for i in range(nsrc)],
-        dsts=[T.qeo[:, 4 * pi:4 * pi + 4] for _ in qd], alu_op=1)], local_sem=S.lsend)
+    nsrc = len(psrc)
+    mask = _common_mask(topo, core, ranks)
+    sent = 0
+    qi = _qserver(h, k)
+    if qi is not None:
+        neng = len(_bits(_common_mask(topo, psrc[0], [core]) & _common_mask(topo, ranks[0], [ranks[1]])))
+        g.wait_ge(S.qarrR, nsrc * neng)
+        g.remote_dma_fused([RemoteDMATransfer(
+            dst_ids=[_did(topo, ranks[qi])], dma_engine_mask=mask, remote_sem=S.qarr,
+            srcs=[T.qlb[i] for i in range(nsrc)], dsts=[T.qg[pi]], alu_op=1)], local_sem=S.lsend)
+        sent += len(_bits(mask))
     order = [ranks[(k + i) % len(ranks)] for i in range(len(ranks))]
     g.wait_ge(S.barr, nsrc)
     g.remote_dma_fused([RemoteDMATransfer(
-        dst_ids=[_did(topo, d) for d in order], dma_engine_mask=_common_mask(topo, core, ranks),
-        remote_sem=(S.garr0 if pi == 0 else S.garr1),
+        dst_ids=[_did(topo, d) for d in order], dma_engine_mask=mask, remote_sem=S["g%d%d" % (pi, h)],
         srcs=[T.lb[i] for i in range(nsrc)],
-        dsts=[T.gg[NCH * pi + k] for _ in order], alu_op=1)], local_sem=S.lsend)
-    g.wait_ge(S.lsend, 2 * len(_bits(_common_mask(topo, core, ranks))))
+        dsts=[T.gg[(2 * pi + h) * NCH + k] for _ in order], alu_op=1)], local_sem=S.lsend)
+    sent += len(_bits(mask))
+    g.wait_ge(S.lsend, sent)
 
 
 def rank_program(g, core, T, topo):
     ranks, planes, pranks, reducers = _layout(T, topo)
     for pi in range(2):
-        if core in reducers[pi]:
-            _reducer(g, core, T, topo, ranks, len(pranks[pi]), pi, reducers[pi].index(core))
-            return
+        for h in range(2):
+            if core in reducers[pi][h]:
+                _reducer(g, core, T, topo, ranks, pranks[pi], pi, h, reducers[pi][h].index(core))
+                return
     if T.rank_of(core) is None:
         return
     S = T.sem
     pi = 0 if core in pranks[0] else 1
     me = pranks[pi].index(core)
     red = reducers[pi]
-    eng = _bits(_common_mask(topo, core, red))
-    H = TK // 2
+    offmask = _common_mask(topo, ranks[0], [ranks[1]])
+    eng = _bits(offmask)
     mult, add = AluOpType.mult, AluOpType.add
 
     g.scalar.dma_start(T.xs[:, 0:H], T.x[:, 0:H]).then_inc(S.x0, 16)
@@ -139,24 +154,32 @@ def rank_program(g, core, T, topo):
     g.vector.wait_ge(S.pq, 4)
     g.vector.tensor_copy(T.qcol[:, :], T.pq[:, 0:4]).then_inc(S.qc, 1)
     g.vector.wait_ge(S.pp0, 1)
-    g.vector.tensor_copy(T.ps[:, 0:H], T.pp0[:, 0:H]).then_inc(S.ps, 1)
+    g.vector.tensor_copy(T.ps[:, 0:H], T.pp0[:, 0:H]).then_inc(S.ps0, 1)
     g.vector.wait_ge(S.pp1, 1)
-    g.vector.tensor_copy(T.ps[:, H:TK], T.pp1[:, 0:H]).then_inc(S.ps, 1)
+    g.vector.tensor_copy(T.ps[:, H:TK], T.pp1[:, 0:H]).then_inc(S.ps1, 1)
 
-    g.wait_ge(S.qc, 1)
+    g.sync.wait_ge(S.qc, 1)
+    g.sync.dma_start(T.qd[:, :], T.qcol[:, :]).then_inc(S.lq1, 16)
+    qto = [red[h][k] for h in range(2) for k in range(NCH) if _qserver(h, k) is not None]
+    g.wait_ge(S.lq1, 16)
     g.remote_dma_fused([RemoteDMATransfer(
-        dst_ids=[_did(topo, red[k])], dma_engine_mask=eng[k], remote_sem=S.qarrR,
-        src=T.qcol[:, :], dst=T.qland[:, 4 * me:4 * me + 4]) for k in range(NCH)], local_sem=S.lsend)
+        dst_ids=[_did(topo, d) for d in qto], dma_engine_mask=offmask, remote_sem=S.qarrR,
+        srcs=[T.qd[:, :]], dsts=[T.qlb[me] for _ in qto])], local_sem=S.lsend)
 
-    g.sync.wait_ge(S.ps, 2)
-    g.sync.dma_start(T.d1[:, :, :], T.ps[:, :]).then_inc(S.l1, 16)
-    g.wait_ge(S.l1, 16)
-    g.remote_dma_fused([RemoteDMATransfer(
-        dst_ids=[_did(topo, red[k])], dma_engine_mask=eng[k], remote_sem=S.barr,
-        src=T.d1[k], dst=T.lb[me]) for k in range(NCH)], local_sem=S.lsend)
+    g.sync.wait_ge(S.ps0, 1)
+    g.sync.dma_start(T.d1[0:NCH], T.ps[:, 0:H]).then_inc(S.l10, 16)
+    g.scalar.wait_ge(S.ps1, 1)
+    g.scalar.dma_start(T.d1[NCH:2 * NCH], T.ps[:, H:TK]).then_inc(S.l11, 16)
+    for h in range(2):
+        g.wait_ge(S["l1%d" % h], 16)
+        g.remote_dma_fused([RemoteDMATransfer(
+            dst_ids=[_did(topo, red[h][k])], dma_engine_mask=eng[k], remote_sem=S.barr,
+            src=T.d1[h * NCH + k], dst=T.lb[me]) for k in range(NCH)], local_sem=S.lsend)
 
-    nq = 2 * len(_bits(_common_mask(topo, reducers[0][0], ranks)))
-    g.vector.wait_ge(S.qarr, nq)
+    g.scalar.wait_ge(S.qarr, 2 * len(eng))
+    g.scalar.dma_start(T.qeo[:, 0:4], T.qg[0]).then_inc(S.lq2, 16)
+    g.scalar.dma_start(T.qeo[:, 4:8], T.qg[1]).then_inc(S.lq2, 16)
+    g.vector.wait_ge(S.lq2, 32)
     g.vector.tensor_tensor(T.qs[:, :], T.qeo[:, 0:4], T.qeo[:, 4:8], add).then_inc(S.c1, 1)
     g.scalar.wait_ge(S.c1, 1)
     g.scalar.activation(T.sq[:, :], T.qs[:, :], ActivationFunctionType.Sqrt, bias=EPS, scale=1.0 / DFEAT).then_inc(S.c2, 1)
@@ -173,16 +196,16 @@ def rank_program(g, core, T, topo):
         g.tensor.matmul(pS[:, 128 * (j % 2):128 * (j % 2) + 128], T.ones[:, :], T.diag[:, 128 * j:128 * j + 128],
                         True, True).then_inc(S.S0 if j < 2 else S.S1, 1)
 
-    ng = NCH * len(_bits(_common_mask(topo, reducers[0][0], ranks)))
-    g.sync.wait_ge(S.garr0, ng)
-    g.sync.dma_start(T.eo[:, 0:TK], T.gg[0:NCH]).then_inc(S.l2a, 16)
-    g.scalar.wait_ge(S.garr1, ng)
-    g.scalar.dma_start(T.eo[:, TK:2 * TK], T.gg[NCH:2 * NCH]).then_inc(S.l2b, 16)
+    ng = NCH * len(eng)
+    for h in range(2):
+        for p, q in ((0, g.sync), (1, g.scalar)):
+            q.wait_ge(S["g%d%d" % (p, h)], ng)
+            q.dma_start(T.eo[:, p * TK + h * H:p * TK + h * H + H],
+                        T.gg[(2 * p + h) * NCH:(2 * p + h + 1) * NCH]).then_inc(S["l2%d" % h], 16)
 
-    g.vector.wait_ge(S.l2a, 16)
-    g.vector.wait_ge(S.l2b, 16)
     for h in range(2):
         lo, hi = h * H, h * H + H
+        g.vector.wait_ge(S["l2%d" % h], 32)
         g.vector.tensor_tensor(T.rr[:, lo:hi], T.eo[:, lo:hi], T.eo[:, TK + lo:TK + hi], add).then_inc(S["a%d" % h], 1)
         g.vector.wait_ge(S["a%d" % h], 1)
         g.vector.wait_ge(S["S%d" % h], 2)
@@ -194,4 +217,4 @@ def rank_program(g, core, T, topo):
     g.scalar.dma_start(T.y[:, H:TK], T.yo[:, H:TK]).then_inc(S.y1, 16)
     g.sync.wait_ge(S.y0, 16)
     g.scalar.wait_ge(S.y1, 16)
-    g.wait_ge(S.lsend, 2 * NCH)
+    g.wait_ge(S.lsend, 3 * len(eng))

@@ -3,43 +3,55 @@ from concourse.mybir import AluOpType, ActivationFunctionType
 
 NR = 12
 TK = 512
-H = TK // 2
 DFEAT = 128 * NR
 EPS = 0.01
 NCH = 8
-CW = H // NCH
+PARTS = [(0, 192), (192, 384), (384, 512)]
+NP = len(PARTS)
+CWS = [(b - a) // NCH for a, b in PARTS]
 
 SCRATCH = {
     "xs": ("sbuf", [128, TK], "float32"),
     "ws": ("sbuf", [128, 128], "float32"),
     "x2": ("sbuf", [128, TK], "float32"),
     "ones": ("sbuf", [128, 128], "float32"),
+    "onesb": ("sbuf", [128, 128], "bfloat16"),
     "ident": ("sbuf", [128, 128], "float32"),
+    "identb": ("sbuf", [128, 128], "bfloat16"),
     "ps": ("sbuf", [128, TK], "float32"),
     "qcol": ("sbuf", [128, 4], "float32"),
+    "aa": ("sbuf", [128, 4], "float32"),
+    "ra": ("sbuf", [128, 4], "float32"),
+    "ra2": ("sbuf", [128, 4], "float32"),
     "qeo": ("sbuf", [128, 8], "float32"),
-    "qs": ("sbuf", [128, 4], "float32"),
+    "qu": ("sbuf", [128, 4], "float32"),
     "sq": ("sbuf", [128, 4], "float32"),
+    "rs": ("sbuf", [128, 4], "float32"),
     "sc": ("sbuf", [128, 4], "float32"),
-    "diag": ("sbuf", [128, TK], "float32"),
+    "hib": ("sbuf", [128, 4], "bfloat16"),
+    "lof": ("sbuf", [128, 4], "float32"),
+    "dgh": ("sbuf", [128, TK], "bfloat16"),
+    "dgl": ("sbuf", [128, TK], "bfloat16"),
     "eo": ("sbuf", [128, 2 * TK], "float32"),
     "rr": ("sbuf", [128, TK], "float32"),
     "yo": ("sbuf", [128, TK], "float32"),
-    "pp0": ("psum", [128, 512], "float32"),
-    "pp1": ("psum", [128, 512], "float32"),
     "pq": ("psum", [128, 512], "float32"),
-    "pS0": ("psum", [128, 512], "float32"),
-    "pS1": ("psum", [128, 512], "float32"),
-    "qd": ("dram", [128, 4], "float32"),
-    "qlb": ("dram", [NCH, 128, 4], "float32"),
-    "qg": ("dram", [2, 128, 4], "float32"),
-    "d1": ("dram", [2 * NCH, 128, CW], "float32"),
-    "lb": ("dram", [NCH, 128, CW], "float32"),
-    "gg": ("dram", [4 * NCH, 128, CW], "float32"),
+    "qd": ("dram", [2, 128, 2], "float32"),
+    "qlb": ("dram", [NCH, 128, 2], "float32"),
+    "qg": ("dram", [4, 128, 2], "float32"),
 }
-SEMAPHORES = ["x0", "x1", "w", "ones", "id", "sq0", "sq1", "pq", "pp0", "pp1", "qc", "lq1", "lq2", "ps0", "ps1",
-              "l10", "l11", "lsend", "qarrR", "barr", "qarr", "g00", "g01", "g10", "g11", "c1", "c2", "c3",
-              "dg0", "dg1", "dg2", "dg3", "S0", "S1", "l20", "l21", "a0", "a1", "m0", "m1", "y0", "y1"]
+for _p in range(NP):
+    SCRATCH["pp%d" % _p] = ("psum", [128, 512], "float32")
+    SCRATCH["d1%d" % _p] = ("dram", [NCH, 128, CWS[_p]], "float32")
+    SCRATCH["lb%d" % _p] = ("dram", [NCH, 128, CWS[_p]], "float32")
+    SCRATCH["gg%d" % _p] = ("dram", [2 * NCH, 128, CWS[_p]], "float32")
+for _j in range(4):
+    SCRATCH["pS%d" % _j] = ("psum", [128, 512], "float32")
+
+SEMAPHORES = (["x", "w", "ones", "onesb", "id", "idb", "sqa", "sqb", "sqc", "pq", "qc", "ea", "e1", "e2", "lq1", "lq2",
+               "lsend", "qarrR", "barr", "qarr", "c2", "c3", "c4", "c5", "c6", "c8"]
+              + ["%s%d" % (n, p) for p in range(NP) for n in ("pp", "ps", "l1", "g0", "g1", "l2", "a", "m", "y")]
+              + ["%s%d" % (n, j) for j in range(4) for n in ("dh", "dl", "S")])
 
 
 def _layout(T, topo):
@@ -52,15 +64,18 @@ def _layout(T, topo):
     pranks = [[r for r in ranks if topo.chip(r) in pl] for pl in planes]
     reducers = []
     for pi, pl in enumerate(planes):
-        halves = [[], []]
+        parts = [[] for _ in range(NP)]
         for k, ch in enumerate(pl):
             cands = [c for c in cores if topo.chip(c) == ch and c not in ranks
                      and all(topo.may_write(c, r) for r in ranks)]
             dies = sorted(set(topo.die(c) for c in cands))
-            for h in range(2):
-                want = dies[(k + pi + h) % len(dies)]
-                halves[h].append([c for c in cands if topo.die(c) == want][0])
-        reducers.append(halves)
+            used = []
+            for p in range(NP):
+                want = dies[(k + pi + p) % len(dies)]
+                c = [c for c in cands if topo.die(c) == want and c not in used][0]
+                used.append(c)
+                parts[p].append(c)
+        reducers.append(parts)
     return ranks, planes, pranks, reducers
 
 
@@ -80,30 +95,30 @@ def _bits(m):
     return [1 << b for b in range(16) if (m >> b) & 1]
 
 
-def _qserver(h, k):
-    i = (1 - h) * NCH + k
-    return i if i < NR else None
+def _qjob(p, k):
+    i = (NP - 1 - p) * NCH + k
+    return (i % NR, i // NR) if i < 2 * NR else None
 
 
-def _reducer(g, core, T, topo, ranks, psrc, pi, h, k):
+def _reducer(g, core, T, topo, ranks, psrc, pi, p, k):
     S = T.sem
     nsrc = len(psrc)
     mask = _common_mask(topo, core, ranks)
     sent = 0
-    qi = _qserver(h, k)
-    if qi is not None:
-        neng = len(_bits(_common_mask(topo, psrc[0], [core]) & _common_mask(topo, ranks[0], [ranks[1]])))
-        g.wait_ge(S.qarrR, nsrc * neng)
+    job = _qjob(p, k)
+    if job is not None:
+        g.wait_ge(S.qarrR, nsrc)
         g.remote_dma_fused([RemoteDMATransfer(
-            dst_ids=[_did(topo, ranks[qi])], dma_engine_mask=mask, remote_sem=S.qarr,
-            srcs=[T.qlb[i] for i in range(nsrc)], dsts=[T.qg[pi]], alu_op=1)], local_sem=S.lsend)
+            dst_ids=[_did(topo, ranks[job[0]])], dma_engine_mask=mask, remote_sem=S.qarr,
+            srcs=[T.qlb[i] for i in range(nsrc)], dsts=[T.qg[2 * pi + job[1]]], alu_op=1)], local_sem=S.lsend)
         sent += len(_bits(mask))
     order = [ranks[(k + i) % len(ranks)] for i in range(len(ranks))]
+    lb, gg = T["lb%d" % p], T["gg%d" % p]
     g.wait_ge(S.barr, nsrc)
     g.remote_dma_fused([RemoteDMATransfer(
-        dst_ids=[_did(topo, d) for d in order], dma_engine_mask=mask, remote_sem=S["g%d%d" % (pi, h)],
-        srcs=[T.lb[i] for i in range(nsrc)],
-        dsts=[T.gg[(2 * pi + h) * NCH + k] for _ in order], alu_op=1)], local_sem=S.lsend)
+        dst_ids=[_did(topo, d) for d in order], dma_engine_mask=mask, remote_sem=S["g%d%d" % (pi, p)],
+        srcs=[lb[i] for i in range(nsrc)],
+        dsts=[gg[pi * NCH + k] for _ in order], alu_op=1)], local_sem=S.lsend)
     sent += len(_bits(mask))
     g.wait_ge(S.lsend, sent)
 
@@ -111,9 +126,9 @@ def _reducer(g, core, T, topo, ranks, psrc, pi, h, k):
 def rank_program(g, core, T, topo):
     ranks, planes, pranks, reducers = _layout(T, topo)
     for pi in range(2):
-        for h in range(2):
-            if core in reducers[pi][h]:
-                _reducer(g, core, T, topo, ranks, pranks[pi], pi, h, reducers[pi][h].index(core))
+        for p in range(NP):
+            if core in reducers[pi][p]:
+                _reducer(g, core, T, topo, ranks, pranks[pi], pi, p, reducers[pi][p].index(core))
                 return
     if T.rank_of(core) is None:
         return
@@ -123,98 +138,132 @@ def rank_program(g, core, T, topo):
     red = reducers[pi]
     offmask = _common_mask(topo, ranks[0], [ranks[1]])
     eng = _bits(offmask)
-    mult, add = AluOpType.mult, AluOpType.add
+    mult, add, sub = AluOpType.mult, AluOpType.add, AluOpType.subtract
+    Sqrt, Square = ActivationFunctionType.Sqrt, ActivationFunctionType.Square
 
-    g.scalar.dma_start(T.xs[:, 0:H], T.x[:, 0:H]).then_inc(S.x0, 16)
-    g.sync.dma_start(T.xs[:, H:TK], T.x[:, H:TK]).then_inc(S.x1, 16)
-    g.scalar.dma_start(T.ws[:, :], T.w[:, :]).then_inc(S.w, 16)
+    g.sync.dma_start(T.xs[:, :], T.x[:, :]).then_inc(S.x, 16)
+    g.sync.dma_start(T.ws[:, :], T.w[:, :]).then_inc(S.w, 16)
 
     g.vector.memset(T.ones[:, :], 1.0).then_inc(S.ones, 1)
+    g.vector.memset(T.onesb[:, :], 1.0).then_inc(S.onesb, 1)
     g.wait_ge(S.ones, 1)
     g.affine_select(T.ident[:, :], T.ones[:, :], [[-1, 128]], AluOpType.is_equal, 0.0, 0, 1).then_inc(S.id, 1)
 
-    g.scalar.wait_ge(S.x0, 16)
-    g.scalar.activation(T.x2[:, 0:H], T.xs[:, 0:H], ActivationFunctionType.Square).then_inc(S.sq0, 1)
-    g.scalar.wait_ge(S.x1, 16)
-    g.scalar.activation(T.x2[:, H:TK], T.xs[:, H:TK], ActivationFunctionType.Square).then_inc(S.sq1, 1)
+    g.scalar.wait_ge(S.x, 16)
+    g.scalar.activation(T.x2[:, 0:128], T.xs[:, 0:128], Square).then_inc(S.sqa, 1)
+    g.scalar.activation(T.x2[:, 128:384], T.xs[:, 128:384], Square).then_inc(S.sqb, 1)
+    g.vector.wait_ge(S.x, 16)
+    g.vector.tensor_tensor(T.x2[:, 384:512], T.xs[:, 384:512], T.xs[:, 384:512], mult).then_inc(S.sqc, 1)
 
     g.tensor.wait_ge(S.ones, 1)
-    for j in range(4):
-        if j == 0:
-            g.tensor.wait_ge(S.sq0, 1)
-        if j == 2:
-            g.tensor.wait_ge(S.sq1, 1)
+    for j, sem in ((0, S.sqa), (3, S.sqc), (1, S.sqb), (2, S.sqb)):
+        g.tensor.wait_ge(sem, 1)
         g.tensor.matmul(T.pq[:, j:j + 1], T.x2[:, 128 * j:128 * j + 128], T.ones[:, 0:1], True, True).then_inc(S.pq, 1)
     g.tensor.wait_ge(S.w, 16)
-    g.tensor.wait_ge(S.x0, 16)
-    g.tensor.matmul(T.pp0[:, 0:H], T.ws[:, :], T.xs[:, 0:H], True, True).then_inc(S.pp0, 1)
-    g.tensor.wait_ge(S.x1, 16)
-    g.tensor.matmul(T.pp1[:, 0:H], T.ws[:, :], T.xs[:, H:TK], True, True).then_inc(S.pp1, 1)
+    g.tensor.wait_ge(S.x, 16)
+    for p, (lo, hi) in enumerate(PARTS):
+        g.tensor.matmul(T["pp%d" % p][:, 0:hi - lo], T.ws[:, :], T.xs[:, lo:hi], True, True).then_inc(S["pp%d" % p], 1)
 
     g.vector.wait_ge(S.pq, 4)
-    g.vector.tensor_copy(T.qcol[:, :], T.pq[:, 0:4]).then_inc(S.qc, 1)
-    g.vector.wait_ge(S.pp0, 1)
-    g.vector.tensor_copy(T.ps[:, 0:H], T.pp0[:, 0:H]).then_inc(S.ps0, 1)
-    g.vector.wait_ge(S.pp1, 1)
-    g.vector.tensor_copy(T.ps[:, H:TK], T.pp1[:, 0:H]).then_inc(S.ps1, 1)
+    g.vector.tensor_scalar(T.qcol[:, :], T.pq[:, 0:4], EPS * DFEAT / NR, None, add).then_inc(S.qc, 1)
+    for p, (lo, hi) in enumerate(PARTS):
+        g.vector.wait_ge(S["pp%d" % p], 1)
+        g.vector.tensor_copy(T.ps[:, lo:hi], T["pp%d" % p][:, 0:hi - lo]).then_inc(S["ps%d" % p], 1)
 
     g.sync.wait_ge(S.qc, 1)
-    g.sync.dma_start(T.qd[:, :], T.qcol[:, :]).then_inc(S.lq1, 16)
-    qto = [red[h][k] for h in range(2) for k in range(NCH) if _qserver(h, k) is not None]
+    g.sync.dma_start(T.qd[0:2], T.qcol[:, :]).then_inc(S.lq1, 16)
+    serv = [[red[p][k] for p in range(NP) for k in range(NCH) if _qjob(p, k) is not None and _qjob(p, k)[1] == c]
+            for c in range(2)]
+    ne = len(eng) // 2
     g.wait_ge(S.lq1, 16)
     g.remote_dma_fused([RemoteDMATransfer(
-        dst_ids=[_did(topo, d) for d in qto], dma_engine_mask=offmask, remote_sem=S.qarrR,
-        srcs=[T.qd[:, :]], dsts=[T.qlb[me] for _ in qto])], local_sem=S.lsend)
+        dst_ids=[_did(topo, d) for d in serv[c][i::ne]], dma_engine_mask=eng[c * ne + i], remote_sem=S.qarrR,
+        srcs=[T.qd[c]], dsts=[T.qlb[me] for _ in serv[c][i::ne]]) for c in range(2) for i in range(ne)],
+        local_sem=S.lsend)
 
-    g.sync.wait_ge(S.ps0, 1)
-    g.sync.dma_start(T.d1[0:NCH], T.ps[:, 0:H]).then_inc(S.l10, 16)
-    g.scalar.wait_ge(S.ps1, 1)
-    g.scalar.dma_start(T.d1[NCH:2 * NCH], T.ps[:, H:TK]).then_inc(S.l11, 16)
-    for h in range(2):
-        g.wait_ge(S["l1%d" % h], 16)
+    g.scalar.wait_ge(S.qc, 1)
+    g.scalar.activation(T.aa[:, :], T.qcol[:, :], Sqrt, scale=float(NR) / DFEAT).then_inc(S.ea, 1)
+
+    for p, (lo, hi) in enumerate(PARTS):
+        g.sync.wait_ge(S["ps%d" % p], 1)
+        g.sync.dma_start(T["d1%d" % p][0:NCH], T.ps[:, lo:hi]).then_inc(S["l1%d" % p], 16)
+    for p in range(NP):
+        g.wait_ge(S["l1%d" % p], 16)
         g.remote_dma_fused([RemoteDMATransfer(
-            dst_ids=[_did(topo, red[h][k])], dma_engine_mask=eng[k], remote_sem=S.barr,
-            src=T.d1[h * NCH + k], dst=T.lb[me]) for k in range(NCH)], local_sem=S.lsend)
+            dst_ids=[_did(topo, red[p][k])], dma_engine_mask=eng[k], remote_sem=S.barr,
+            src=T["d1%d" % p][k], dst=T["lb%d" % p][me]) for k in range(NCH)], local_sem=S.lsend)
 
-    g.scalar.wait_ge(S.qarr, 2 * len(eng))
-    g.scalar.dma_start(T.qeo[:, 0:4], T.qg[0]).then_inc(S.lq2, 16)
-    g.scalar.dma_start(T.qeo[:, 4:8], T.qg[1]).then_inc(S.lq2, 16)
-    g.vector.wait_ge(S.lq2, 32)
-    g.vector.tensor_tensor(T.qs[:, :], T.qeo[:, 0:4], T.qeo[:, 4:8], add).then_inc(S.c1, 1)
-    g.scalar.wait_ge(S.c1, 1)
-    g.scalar.activation(T.sq[:, :], T.qs[:, :], ActivationFunctionType.Sqrt, bias=EPS, scale=1.0 / DFEAT).then_inc(S.c2, 1)
-    g.vector.wait_ge(S.c2, 1)
-    g.vector.reciprocal(T.sc[:, :], T.sq[:, :]).then_inc(S.c3, 1)
-    g.vector.wait_ge(S.c3, 1)
     g.vector.wait_ge(S.id, 1)
+    g.vector.tensor_copy(T.identb[:, :], T.ident[:, :]).then_inc(S.idb, 1)
+    g.vector.wait_ge(S.ea, 1)
+    g.vector.reciprocal(T.ra[:, :], T.aa[:, :]).then_inc(S.e1, 1)
+    g.vector.wait_ge(S.e1, 1)
+    g.vector.tensor_tensor(T.ra2[:, :], T.ra[:, :], T.ra[:, :], mult).then_inc(S.e2, 1)
+
+    g.sync.wait_ge(S.qarr, 4 * len(eng))
+    g.sync.dma_start(T.qeo[:, 0:4], T.qg[0:2]).then_inc(S.lq2, 16)
+    g.scalar.wait_ge(S.qarr, 4 * len(eng))
+    g.scalar.dma_start(T.qeo[:, 4:8], T.qg[2:4]).then_inc(S.lq2, 16)
+    g.vector.wait_ge(S.e2, 1)
+    g.vector.wait_ge(S.lq2, 32)
     for j in range(4):
-        g.vector.tensor_scalar(T.diag[:, 128 * j:128 * j + 128], T.ident[:, :], T.sc[:, j:j + 1], None,
-                               mult).then_inc(S["dg%d" % j], 1)
+        g.vector.tensor_scalar(T.qu[:, j:j + 1], T.qeo[:, j:j + 1], T.qeo[:, 4 + j:5 + j], T.ra2[:, j:j + 1],
+                               add, mult).then_inc(S.c2, 1)
+    g.scalar.wait_ge(S.c2, 4)
+    g.scalar.activation(T.sq[:, :], T.qu[:, :], Sqrt, scale=1.0 / DFEAT).then_inc(S.c3, 1)
+    g.vector.wait_ge(S.c3, 1)
+    g.vector.reciprocal(T.rs[:, :], T.sq[:, :]).then_inc(S.c4, 1)
+    g.vector.wait_ge(S.c4, 1)
+    g.vector.tensor_tensor(T.sc[:, :], T.rs[:, :], T.ra[:, :], mult).then_inc(S.c5, 1)
+    g.vector.tensor_tensor(T.hib[:, :], T.rs[:, :], T.ra[:, :], mult).then_inc(S.c6, 1)
+
+    g.vector.wait_ge(S.c5, 1)
+    g.vector.wait_ge(S.c6, 1)
+    g.vector.wait_ge(S.idb, 1)
     for j in range(4):
-        g.tensor.wait_ge(S["dg%d" % j], 1)
-        pS = T.pS0 if j < 2 else T.pS1
-        g.tensor.matmul(pS[:, 128 * (j % 2):128 * (j % 2) + 128], T.ones[:, :], T.diag[:, 128 * j:128 * j + 128],
-                        True, True).then_inc(S.S0 if j < 2 else S.S1, 1)
+        g.vector.tensor_scalar(T.lof[:, j:j + 1], T.sc[:, j:j + 1], T.hib[:, j:j + 1], None, sub).then_inc(S.c8, 1)
+    for j in range(4):
+        g.vector.tensor_scalar(T.dgh[:, 128 * j:128 * j + 128], T.identb[:, :], T.sc[:, j:j + 1], None,
+                               mult).then_inc(S["dh%d" % j], 1)
+    g.vector.wait_ge(S.c8, 4)
+    for j in range(4):
+        g.vector.tensor_scalar(T.dgl[:, 128 * j:128 * j + 128], T.identb[:, :], T.lof[:, j:j + 1], None,
+                               mult).then_inc(S["dl%d" % j], 1)
+    g.tensor.wait_ge(S.onesb, 1)
+    for j in range(4):
+        g.tensor.wait_ge(S["dh%d" % j], 1)
+        g.tensor.matmul(T["pS%d" % j][:, 0:128], T.onesb[:, :], T.dgh[:, 128 * j:128 * j + 128], True, False)
+    for j in range(4):
+        g.tensor.wait_ge(S["dl%d" % j], 1)
+        g.tensor.matmul(T["pS%d" % j][:, 0:128], T.onesb[:, :], T.dgl[:, 128 * j:128 * j + 128], False,
+                        True).then_inc(S["S%d" % j], 1)
 
     ng = NCH * len(eng)
-    for h in range(2):
-        for p, q in ((0, g.sync), (1, g.scalar)):
-            q.wait_ge(S["g%d%d" % (p, h)], ng)
-            q.dma_start(T.eo[:, p * TK + h * H:p * TK + h * H + H],
-                        T.gg[(2 * p + h) * NCH:(2 * p + h + 1) * NCH]).then_inc(S["l2%d" % h], 16)
+    for p, (lo, hi) in enumerate(PARTS):
+        for pl, q in ((0, g.sync), (1, g.scalar)):
+            q.wait_ge(S["g%d%d" % (pl, p)], ng)
+            q.dma_start(T.eo[:, pl * TK + lo:pl * TK + hi],
+                        T["gg%d" % p][pl * NCH:(pl + 1) * NCH]).then_inc(S["l2%d" % p], 16)
 
-    for h in range(2):
-        lo, hi = h * H, h * H + H
-        g.vector.wait_ge(S["l2%d" % h], 32)
-        g.vector.tensor_tensor(T.rr[:, lo:hi], T.eo[:, lo:hi], T.eo[:, TK + lo:TK + hi], add).then_inc(S["a%d" % h], 1)
-        g.vector.wait_ge(S["a%d" % h], 1)
-        g.vector.wait_ge(S["S%d" % h], 2)
-        g.vector.tensor_tensor(T.yo[:, lo:hi], T.rr[:, lo:hi], (T.pS0 if h == 0 else T.pS1)[:, 0:H],
-                               mult).then_inc(S["m%d" % h], 1)
-    g.sync.wait_ge(S.m0, 1)
-    g.sync.dma_start(T.y[:, 0:H], T.yo[:, 0:H]).then_inc(S.y0, 16)
-    g.scalar.wait_ge(S.m1, 1)
-    g.scalar.dma_start(T.y[:, H:TK], T.yo[:, H:TK]).then_inc(S.y1, 16)
-    g.sync.wait_ge(S.y0, 16)
-    g.scalar.wait_ge(S.y1, 16)
-    g.wait_ge(S.lsend, 3 * len(eng))
+    nseg = []
+    for p, (lo, hi) in enumerate(PARTS):
+        g.vector.wait_ge(S["l2%d" % p], 32)
+        g.vector.tensor_tensor(T.rr[:, lo:hi], T.eo[:, lo:hi], T.eo[:, TK + lo:TK + hi], add).then_inc(S["a%d" % p], 1)
+        g.vector.wait_ge(S["a%d" % p], 1)
+        n, a = 0, lo
+        while a < hi:
+            j = a // 128
+            b = min(hi, 128 * j + 128)
+            g.vector.wait_ge(S["S%d" % j], 1)
+            g.vector.tensor_tensor(T.yo[:, a:b], T.rr[:, a:b], T["pS%d" % j][:, a - 128 * j:b - 128 * j],
+                                   mult).then_inc(S["m%d" % p], 1)
+            n, a = n + 1, b
+        nseg.append(n)
+    for p, (lo, hi) in enumerate(PARTS):
+        q = g.scalar if p % 2 else g.sync
+        q.wait_ge(S["m%d" % p], nseg[p])
+        q.dma_start(T.y[:, lo:hi], T.yo[:, lo:hi]).then_inc(S["y%d" % p], 16)
+    for p in range(NP):
+        q = g.scalar if p % 2 else g.sync
+        q.wait_ge(S["y%d" % p], 16)
+    g.wait_ge(S.lsend, (1 + NP) * len(eng))

from concourse.bass import DstId, RemoteDMATransfer
from concourse.mybir import AluOpType, ActivationFunctionType

NR = 12
TK = 512
DFEAT = 128 * NR
EPS = 0.01
NCH = 8
PARTS = [(0, 192), (192, 384), (384, 512)]
NP = len(PARTS)
CWS = [(b - a) // NCH for a, b in PARTS]

SCRATCH = {
    "xs": ("sbuf", [128, TK], "float32"),
    "ws": ("sbuf", [128, 128], "float32"),
    "x2": ("sbuf", [128, TK], "float32"),
    "ones": ("sbuf", [128, 128], "float32"),
    "onesb": ("sbuf", [128, 128], "bfloat16"),
    "ident": ("sbuf", [128, 128], "float32"),
    "identb": ("sbuf", [128, 128], "bfloat16"),
    "ps": ("sbuf", [128, TK], "float32"),
    "qcol": ("sbuf", [128, 4], "float32"),
    "aa": ("sbuf", [128, 4], "float32"),
    "ra": ("sbuf", [128, 4], "float32"),
    "ra2": ("sbuf", [128, 4], "float32"),
    "qeo": ("sbuf", [128, 8], "float32"),
    "qu": ("sbuf", [128, 4], "float32"),
    "sq": ("sbuf", [128, 4], "float32"),
    "rs": ("sbuf", [128, 4], "float32"),
    "sc": ("sbuf", [128, 4], "float32"),
    "hib": ("sbuf", [128, 4], "bfloat16"),
    "lof": ("sbuf", [128, 4], "float32"),
    "dgh": ("sbuf", [128, TK], "bfloat16"),
    "dgl": ("sbuf", [128, TK], "bfloat16"),
    "eo": ("sbuf", [128, 2 * TK], "float32"),
    "rr": ("sbuf", [128, TK], "float32"),
    "yo": ("sbuf", [128, TK], "float32"),
    "pq": ("psum", [128, 512], "float32"),
    "qd": ("dram", [2, 128, 2], "float32"),
    "qlb": ("dram", [NCH, 128, 2], "float32"),
    "qg": ("dram", [4, 128, 2], "float32"),
}
for _p in range(NP):
    SCRATCH["pp%d" % _p] = ("psum", [128, 512], "float32")
    SCRATCH["d1%d" % _p] = ("dram", [NCH, 128, CWS[_p]], "float32")
    SCRATCH["lb%d" % _p] = ("dram", [NCH, 128, CWS[_p]], "float32")
    SCRATCH["gg%d" % _p] = ("dram", [2 * NCH, 128, CWS[_p]], "float32")
for _j in range(4):
    SCRATCH["pS%d" % _j] = ("psum", [128, 512], "float32")

SEMAPHORES = (["x", "w", "ones", "onesb", "id", "idb", "sqa", "sqb", "sqc", "pq", "qc", "ea", "e1", "e2", "lq1", "lq2",
               "lsend", "qarrR", "barr", "qarr", "c2", "c3", "c4", "c5", "c6", "c8"]
              + ["%s%d" % (n, p) for p in range(NP) for n in ("pp", "ps", "l1", "g0", "g1", "l2", "a", "m", "y")]
              + ["%s%d" % (n, j) for j in range(4) for n in ("dh", "dl", "S")])


def _layout(T, topo):
    ranks = list(T.cores)
    cores = list(range(topo.CHIPS * topo.CORES_PER_CHIP))
    chips = sorted(set(topo.chip(c) for c in cores))
    c0 = topo.chip(ranks[0])
    first = [ch for ch in chips if ch == c0 or topo.same_plane(ch, c0)]
    planes = [first, [ch for ch in chips if ch not in first]]
    pranks = [[r for r in ranks if topo.chip(r) in pl] for pl in planes]
    reducers = []
    for pi, pl in enumerate(planes):
        parts = [[] for _ in range(NP)]
        for k, ch in enumerate(pl):
            cands = [c for c in cores if topo.chip(c) == ch and c not in ranks
                     and all(topo.may_write(c, r) for r in ranks)]
            dies = sorted(set(topo.die(c) for c in cands))
            used = []
            for p in range(NP):
                want = dies[(k + pi + p) % len(dies)]
                c = [c for c in cands if topo.die(c) == want and c not in used][0]
                used.append(c)
                parts[p].append(c)
        reducers.append(parts)
    return ranks, planes, pranks, reducers


def _did(topo, c):
    rid, pid, _se = topo.addr(c)
    return DstId(rid=rid, pnc=pid)


def _common_mask(topo, src, dsts):
    m = topo.mask(src, dsts[0])
    for d in dsts[1:]:
        m &= topo.mask(src, d)
    return m


def _bits(m):
    return [1 << b for b in range(16) if (m >> b) & 1]


def _qjob(p, k):
    i = (NP - 1 - p) * NCH + k
    return (i % NR, i // NR) if i < 2 * NR else None


def _reducer(g, core, T, topo, ranks, psrc, pi, p, k):
    S = T.sem
    nsrc = len(psrc)
    mask = _common_mask(topo, core, ranks)
    sent = 0
    job = _qjob(p, k)
    if job is not None:
        g.wait_ge(S.qarrR, nsrc)
        g.remote_dma_fused([RemoteDMATransfer(
            dst_ids=[_did(topo, ranks[job[0]])], dma_engine_mask=mask, remote_sem=S.qarr,
            srcs=[T.qlb[i] for i in range(nsrc)], dsts=[T.qg[2 * pi + job[1]]], alu_op=1)], local_sem=S.lsend)
        sent += len(_bits(mask))
    order = [ranks[(k + i) % len(ranks)] for i in range(len(ranks))]
    lb, gg = T["lb%d" % p], T["gg%d" % p]
    g.wait_ge(S.barr, nsrc)
    g.remote_dma_fused([RemoteDMATransfer(
        dst_ids=[_did(topo, d) for d in order], dma_engine_mask=mask, remote_sem=S["g%d%d" % (pi, p)],
        srcs=[lb[i] for i in range(nsrc)],
        dsts=[gg[pi * NCH + k] for _ in order], alu_op=1)], local_sem=S.lsend)
    sent += len(_bits(mask))
    g.wait_ge(S.lsend, sent)


def rank_program(g, core, T, topo):
    ranks, planes, pranks, reducers = _layout(T, topo)
    for pi in range(2):
        for p in range(NP):
            if core in reducers[pi][p]:
                _reducer(g, core, T, topo, ranks, pranks[pi], pi, p, reducers[pi][p].index(core))
                return
    if T.rank_of(core) is None:
        return
    S = T.sem
    pi = 0 if core in pranks[0] else 1
    me = pranks[pi].index(core)
    red = reducers[pi]
    offmask = _common_mask(topo, ranks[0], [ranks[1]])
    eng = _bits(offmask)
    mult, add, sub = AluOpType.mult, AluOpType.add, AluOpType.subtract
    Sqrt, Square = ActivationFunctionType.Sqrt, ActivationFunctionType.Square

    g.sync.dma_start(T.xs[:, :], T.x[:, :]).then_inc(S.x, 16)
    g.sync.dma_start(T.ws[:, :], T.w[:, :]).then_inc(S.w, 16)

    g.vector.memset(T.ones[:, :], 1.0).then_inc(S.ones, 1)
    g.vector.memset(T.onesb[:, :], 1.0).then_inc(S.onesb, 1)
    g.wait_ge(S.ones, 1)
    g.affine_select(T.ident[:, :], T.ones[:, :], [[-1, 128]], AluOpType.is_equal, 0.0, 0, 1).then_inc(S.id, 1)

    g.scalar.wait_ge(S.x, 16)
    g.scalar.activation(T.x2[:, 0:128], T.xs[:, 0:128], Square).then_inc(S.sqa, 1)
    g.scalar.activation(T.x2[:, 128:384], T.xs[:, 128:384], Square).then_inc(S.sqb, 1)
    g.vector.wait_ge(S.x, 16)
    g.vector.tensor_tensor(T.x2[:, 384:512], T.xs[:, 384:512], T.xs[:, 384:512], mult).then_inc(S.sqc, 1)

    g.tensor.wait_ge(S.ones, 1)
    for j, sem in ((0, S.sqa), (3, S.sqc), (1, S.sqb), (2, S.sqb)):
        g.tensor.wait_ge(sem, 1)
        g.tensor.matmul(T.pq[:, j:j + 1], T.x2[:, 128 * j:128 * j + 128], T.ones[:, 0:1], True, True).then_inc(S.pq, 1)
    g.tensor.wait_ge(S.w, 16)
    g.tensor.wait_ge(S.x, 16)
    for p, (lo, hi) in enumerate(PARTS):
        g.tensor.matmul(T["pp%d" % p][:, 0:hi - lo], T.ws[:, :], T.xs[:, lo:hi], True, True).then_inc(S["pp%d" % p], 1)

    g.vector.wait_ge(S.pq, 4)
    g.vector.tensor_scalar(T.qcol[:, :], T.pq[:, 0:4], EPS * DFEAT / NR, None, add).then_inc(S.qc, 1)
    for p, (lo, hi) in enumerate(PARTS):
        g.vector.wait_ge(S["pp%d" % p], 1)
        g.vector.tensor_copy(T.ps[:, lo:hi], T["pp%d" % p][:, 0:hi - lo]).then_inc(S["ps%d" % p], 1)

    g.sync.wait_ge(S.qc, 1)
    g.sync.dma_start(T.qd[0:2], T.qcol[:, :]).then_inc(S.lq1, 16)
    serv = [[red[p][k] for p in range(NP) for k in range(NCH) if _qjob(p, k) is not None and _qjob(p, k)[1] == c]
            for c in range(2)]
    ne = len(eng) // 2
    g.wait_ge(S.lq1, 16)
    g.remote_dma_fused([RemoteDMATransfer(
        dst_ids=[_did(topo, d) for d in serv[c][i::ne]], dma_engine_mask=eng[c * ne + i], remote_sem=S.qarrR,
        srcs=[T.qd[c]], dsts=[T.qlb[me] for _ in serv[c][i::ne]]) for c in range(2) for i in range(ne)],
        local_sem=S.lsend)

    g.scalar.wait_ge(S.qc, 1)
    g.scalar.activation(T.aa[:, :], T.qcol[:, :], Sqrt, scale=float(NR) / DFEAT).then_inc(S.ea, 1)

    for p, (lo, hi) in enumerate(PARTS):
        g.sync.wait_ge(S["ps%d" % p], 1)
        g.sync.dma_start(T["d1%d" % p][0:NCH], T.ps[:, lo:hi]).then_inc(S["l1%d" % p], 16)
    for p in range(NP):
        g.wait_ge(S["l1%d" % p], 16)
        g.remote_dma_fused([RemoteDMATransfer(
            dst_ids=[_did(topo, red[p][k])], dma_engine_mask=eng[k], remote_sem=S.barr,
            src=T["d1%d" % p][k], dst=T["lb%d" % p][me]) for k in range(NCH)], local_sem=S.lsend)

    g.vector.wait_ge(S.id, 1)
    g.vector.tensor_copy(T.identb[:, :], T.ident[:, :]).then_inc(S.idb, 1)
    g.vector.wait_ge(S.ea, 1)
    g.vector.reciprocal(T.ra[:, :], T.aa[:, :]).then_inc(S.e1, 1)
    g.vector.wait_ge(S.e1, 1)
    g.vector.tensor_tensor(T.ra2[:, :], T.ra[:, :], T.ra[:, :], mult).then_inc(S.e2, 1)

    g.sync.wait_ge(S.qarr, 4 * len(eng))
    g.sync.dma_start(T.qeo[:, 0:4], T.qg[0:2]).then_inc(S.lq2, 16)
    g.scalar.wait_ge(S.qarr, 4 * len(eng))
    g.scalar.dma_start(T.qeo[:, 4:8], T.qg[2:4]).then_inc(S.lq2, 16)
    g.vector.wait_ge(S.e2, 1)
    g.vector.wait_ge(S.lq2, 32)
    for j in range(4):
        g.vector.tensor_scalar(T.qu[:, j:j + 1], T.qeo[:, j:j + 1], T.qeo[:, 4 + j:5 + j], T.ra2[:, j:j + 1],
                               add, mult).then_inc(S.c2, 1)
    g.scalar.wait_ge(S.c2, 4)
    g.scalar.activation(T.sq[:, :], T.qu[:, :], Sqrt, scale=1.0 / DFEAT).then_inc(S.c3, 1)
    g.vector.wait_ge(S.c3, 1)
    g.vector.reciprocal(T.rs[:, :], T.sq[:, :]).then_inc(S.c4, 1)
    g.vector.wait_ge(S.c4, 1)
    g.vector.tensor_tensor(T.sc[:, :], T.rs[:, :], T.ra[:, :], mult).then_inc(S.c5, 1)
    g.vector.tensor_tensor(T.hib[:, :], T.rs[:, :], T.ra[:, :], mult).then_inc(S.c6, 1)

    g.vector.wait_ge(S.c5, 1)
    g.vector.wait_ge(S.c6, 1)
    g.vector.wait_ge(S.idb, 1)
    for j in range(4):
        g.vector.tensor_scalar(T.lof[:, j:j + 1], T.sc[:, j:j + 1], T.hib[:, j:j + 1], None, sub).then_inc(S.c8, 1)
    for j in range(4):
        g.vector.tensor_scalar(T.dgh[:, 128 * j:128 * j + 128], T.identb[:, :], T.sc[:, j:j + 1], None,
                               mult).then_inc(S["dh%d" % j], 1)
    g.vector.wait_ge(S.c8, 4)
    for j in range(4):
        g.vector.tensor_scalar(T.dgl[:, 128 * j:128 * j + 128], T.identb[:, :], T.lof[:, j:j + 1], None,
                               mult).then_inc(S["dl%d" % j], 1)
    g.tensor.wait_ge(S.onesb, 1)
    for j in range(4):
        g.tensor.wait_ge(S["dh%d" % j], 1)
        g.tensor.matmul(T["pS%d" % j][:, 0:128], T.onesb[:, :], T.dgh[:, 128 * j:128 * j + 128], True, False)
    for j in range(4):
        g.tensor.wait_ge(S["dl%d" % j], 1)
        g.tensor.matmul(T["pS%d" % j][:, 0:128], T.onesb[:, :], T.dgl[:, 128 * j:128 * j + 128], False,
                        True).then_inc(S["S%d" % j], 1)

    ng = NCH * len(eng)
    for p, (lo, hi) in enumerate(PARTS):
        for pl, q in ((0, g.sync), (1, g.scalar)):
            q.wait_ge(S["g%d%d" % (pl, p)], ng)
            q.dma_start(T.eo[:, pl * TK + lo:pl * TK + hi],
                        T["gg%d" % p][pl * NCH:(pl + 1) * NCH]).then_inc(S["l2%d" % p], 16)

    nseg = []
    for p, (lo, hi) in enumerate(PARTS):
        g.vector.wait_ge(S["l2%d" % p], 32)
        g.vector.tensor_tensor(T.rr[:, lo:hi], T.eo[:, lo:hi], T.eo[:, TK + lo:TK + hi], add).then_inc(S["a%d" % p], 1)
        g.vector.wait_ge(S["a%d" % p], 1)
        n, a = 0, lo
        while a < hi:
            j = a // 128
            b = min(hi, 128 * j + 128)
            g.vector.wait_ge(S["S%d" % j], 1)
            g.vector.tensor_tensor(T.yo[:, a:b], T.rr[:, a:b], T["pS%d" % j][:, a - 128 * j:b - 128 * j],
                                   mult).then_inc(S["m%d" % p], 1)
            n, a = n + 1, b
        nseg.append(n)
    for p, (lo, hi) in enumerate(PARTS):
        q = g.scalar if p % 2 else g.sync
        q.wait_ge(S["m%d" % p], nseg[p])
        q.dma_start(T.y[:, lo:hi], T.yo[:, lo:hi]).then_inc(S["y%d" % p], 16)
    for p in range(NP):
        q = g.scalar if p % 2 else g.sync
        q.wait_ge(S["y%d" % p], 16)
    g.wait_ge(S.lsend, (1 + NP) * len(eng))
